import numpy as np
import ml_dtypes


def mxq(x, axis, fmt="e4m3"):
    dtype, down = {"e4m3": (ml_dtypes.float8_e4m3fn, 7), "e5m2": (ml_dtypes.float8_e5m2, 14)}[fmt]
    v = np.moveaxis(np.asarray(x, np.float32).astype(ml_dtypes.bfloat16).astype(np.float64), axis, -1)
    blocks = v.reshape(v.shape[:-1] + (-1, 32))
    amax = np.abs(blocks).max(-1, keepdims=True)
    byte = np.maximum(np.where(amax > 0, np.frexp(amax)[1] - 1 + 127, 0) - down, 1)
    scale = np.exp2(byte - 127.0)
    codes = (blocks / scale).astype(np.float32).astype(dtype).astype(np.float64)
    return np.moveaxis((codes * scale).reshape(v.shape), -1, axis)


WIDE = False


def mx_kscale(k):
    if not WIDE:
        return np.ones(k)
    levels = np.array([10, -10, 5, -5, 0])
    if k % 512:
        return np.exp2(np.random.permutation(np.resize(levels, k // 32))).repeat(32)
    a = np.empty((k // 512, 16))
    for p in range(k // 512):
        a[p, :8] = np.random.permutation(np.resize(levels, 8))
        for g in range(8):
            far = levels[np.abs(levels - a[p, g]) >= 10]
            a[p, g + 8] = far[np.random.randint(len(far))]
    return np.exp2(a.ravel()).repeat(32)


def f64(x):
    return np.asarray(x).astype(np.float64)


def striped8(idx):
    return np.asarray(idx).reshape(8, -1, 16).transpose(0, 2, 1).reshape(128, -1).astype(np.uint16)


def unstriped8(offs):
    return offs.reshape(8, 16, -1).transpose(0, 2, 1).reshape(8, -1).astype(np.int64)


def pick8(x, idx, run):
    r = np.arange(len(x))
    return x[r[:, None], idx[r % (8 * run) // run]]


E2M1 = np.array([0.0, 0.5, 1.0, 1.5, 2.0, 3.0, 4.0, 6.0, -0.0, -0.5, -1.0, -1.5, -2.0, -3.0, -4.0, -6.0])


def pack_weight(w, fmt):
    k, n = w.shape
    w = f64(np.asarray(w, np.float32).astype(ml_dtypes.bfloat16)).reshape(k // 32, 32, n)
    amax = np.abs(w).max(1)
    if fmt == "e4m3":
        byte = np.frexp(amax)[1] - 1 + 127 - 7
    else:
        mant, ex = np.frexp(amax / 6.0)
        byte = np.where(mant > 0.5, ex, ex - 1) + 127
    byte = np.clip(np.where(amax > 0, byte, 1), 1, 254)
    scaled = (w * np.exp2(127.0 - byte)[:, None, :]).reshape(k, n).astype(np.float32)
    by_word = np.ascontiguousarray(scaled.reshape(k // 512, 128, 4, n).transpose(0, 1, 3, 2))
    if fmt == "e4m3":
        words = by_word.astype(ml_dtypes.float8_e4m3fn).view(np.uint8)
    else:
        c = by_word.astype(ml_dtypes.float4_e2m1fn).view(np.uint8) & 0xF
        words = (c[..., 0::2] | (c[..., 1::2] << 4)).reshape(k // 512, 128, 2 * n)
    return np.ascontiguousarray(words), np.ascontiguousarray(byte.astype(np.uint8).reshape(k // 512, 16, n))


def unpack_weight(words, scales, fmt):
    g, _, n = scales.shape
    words = np.ascontiguousarray(words).reshape(g, 128, n, -1)
    if fmt == "e4m3":
        vals = words.view(ml_dtypes.float8_e4m3fn).astype(np.float64)
    else:
        nib = np.empty((g, 128, n, 4), np.uint8)
        nib[..., 0::2] = words & 0xF
        nib[..., 1::2] = words >> 4
        vals = E2M1[nib]
    vals = vals * np.repeat(np.exp2(scales.astype(np.float64) - 127.0), 8, axis=1)[..., None]
    return vals.transpose(0, 1, 3, 2).reshape(g * 512, n)


D, T, I, Q = 512, 1024, 512, 128


def setup_inputs():
    n = np.random.standard_normal
    idx = np.stack([np.random.permutation(T)[:I] for _ in range(8)])
    idx2 = np.stack([np.random.permutation(T)[:I] for _ in range(8)])
    idx3 = np.stack([np.random.permutation(T)[:I] for _ in range(8)])
    idx4 = np.stack([np.random.permutation(T)[:I] for _ in range(8)])
    fd = mx_kscale(D)
    keysp = pack_weight(n((D, T)) / fd[:, None], "e4m3")
    tagsp = pack_weight(n((D, T)) / fd[:, None], "e2m1")
    return {
        "query": (n((D, Q)) * 0.75 / np.sqrt(D) * fd[:, None]).astype(np.float32),
        "query2": (n((D, Q)) * 0.75 / np.sqrt(D) * fd[:, None]).astype(np.float32),
        "keys_words": keysp[0],
        "keys_scales": keysp[1],
        "tags_words": tagsp[0],
        "tags_scales": tagsp[1],
        "lam": (np.random.uniform(0.5, 1.5, (Q, 1))).astype(np.float32),
        "offs": striped8(idx),
        "offs2": striped8(idx2),
        "offs3": striped8(idx3),
        "offs4": striped8(idx4),
    }


def reference(query, query2, keys_words, keys_scales, tags_words, tags_scales, lam, offs, offs2, offs3, offs4):
    idx = unstriped8(offs)
    idx2 = unstriped8(offs2)
    idx3 = unstriped8(offs3)
    idx4 = unstriped8(offs4)
    keysu = unpack_weight(keys_words, keys_scales, "e4m3")
    tagsu = unpack_weight(tags_words, tags_scales, "e2m1")
    queryq = mxq(f64(query), 0, "e4m3")
    query2q = mxq(f64(query2), 0, "e4m3")
    a = queryq.T @ keysu + query2q.T @ tagsu
    w = np.maximum(pick8(a, idx2, 16), pick8(a, idx3, 16))
    f1 = np.zeros((Q, T))
    f1[np.arange(Q)[:, None], idx[np.arange(Q) % 128 // 16]] = w
    cc = a - f1 * f64(lam)
    tc2 = np.max(cc, axis=1, keepdims=True)
    y = np.exp(pick8(cc, idx4, 16) - tc2)
    return y

@@ -1,0 +1,141 @@
+from contextlib import ExitStack
+
+import concourse.mybir as mybir
+
+F32 = mybir.dt.float32
+BF16 = mybir.dt.bfloat16
+I32 = mybir.dt.int32
+U32 = mybir.dt.uint32
+U16 = mybir.dt.uint16
+U8 = mybir.dt.uint8
+FP8X4 = mybir.dt.float8_e4m3fn_x4
+FP4X4 = mybir.dt.float4_e2m1fn_x4
+ALU = mybir.AluOpType
+ACT = mybir.ActivationFunctionType
+
+P = 128
+D, T, SLOTS, Q = 512, 1024, 512, 128
+PACK = 4
+BANK = 256
+HALF = SLOTS // 2
+FLOPS = 2 * 2 * D * Q * T
+
+
+def load_scale_rows(nc, plane, rows):
+    for quad in range(4):
+        nc.sync.dma_start(
+            out=plane[32 * quad : 32 * quad + 4, :].bitcast(I32),
+            in_=rows[0, 4 * quad : 4 * quad + 4, :].bitcast(I32),
+        )
+
+
+def quantise_queries(nc, pool, raw, name):
+    grouped = pool.tile([P, Q, PACK], BF16, align_bytes=64, name=name + "_bf16")
+    codes = pool.tile([P, Q], U32, align_bytes=64, name=name + "_codes")
+    scales = pool.tile([P, Q], U8, align_bytes=64, name=name + "_scales")
+    nc.vector.tensor_copy(
+        out=grouped[:].rearrange("p (c i) t -> p c t i", i=4),
+        in_=raw[:].rearrange("p t (c i) -> p c t i", i=4),
+    )
+    nc.vector.quantize_mx(
+        out=codes[:].bitcast(FP8X4), scales=scales[:], in_=grouped[:].rearrange("p c t -> p (c t)")
+    )
+    return codes, scales
+
+
+def tile_attend_shadowed_parts_kernel(
+    tc, query, query2, keys_words, keys_scales, tags_words, tags_scales, lam, offs, offs2, offs3, offs4, out
+):
+    nc = tc.nc
+    with ExitStack() as ctx:
+        pool = ctx.enter_context(tc.tile_pool(name="sbuf", bufs=1))
+        psum = ctx.enter_context(tc.psum_pool(name="psum", bufs=1))
+
+        tags_plane = pool.tile([P, T], U8, align_bytes=64)
+        keys_plane = pool.tile([P, T], U8, align_bytes=64)
+        shadow = pool.tile([P, T], F32)
+        nc.vector.memset(tags_plane[:].bitcast(I32), 0)
+        nc.vector.memset(keys_plane[:].bitcast(I32), 0)
+        nc.vector.memset(shadow[:], 0.0)
+
+        query_raw = pool.tile([P, PACK, Q], F32)
+        query2_raw = pool.tile([P, PACK, Q], F32)
+        tags = pool.tile([P, 2 * T], U8, align_bytes=64)
+        keys = [pool.tile([P, T // 2], U32, align_bytes=64, name=f"keys{h}") for h in range(2)]
+        keys_dram = keys_words[0].rearrange("p n t -> p (n t)").bitcast(I32)
+        lists = [pool.tile([P, SLOTS // 16], U16, name=f"list{n}") for n in range(4)]
+        own_list, left_list, right_list, out_list = lists
+        lam_col = pool.tile([P, 1], F32)
+
+        nc.sync.dma_start(out=query2_raw[:], in_=query2.rearrange("(p t) c -> p t c", t=PACK))
+        nc.sync.dma_start(out=tags[:].bitcast(I32), in_=tags_words[0].bitcast(I32))
+        load_scale_rows(nc, tags_plane, tags_scales)
+        nc.sync.dma_start(out=query_raw[:], in_=query.rearrange("(p t) c -> p t c", t=PACK))
+        nc.sync.dma_start(out=keys[0][:].bitcast(I32), in_=keys_dram[:, : T // 2])
+        load_scale_rows(nc, keys_plane, keys_scales)
+        nc.sync.dma_start(out=keys[1][:].bitcast(I32), in_=keys_dram[:, T // 2 :])
+        nc.sync.dma_start(left_list[:], offs2)
+        nc.sync.dma_start(right_list[:], offs3)
+        nc.sync.dma_start(own_list[:], offs)
+        nc.sync.dma_start(out_list[:], offs4)
+        nc.sync.dma_start(out=lam_col[:], in_=lam)
+
+        q2_codes, q2_scales = quantise_queries(nc, pool, query2_raw, "query2")
+        q_codes, q_scales = quantise_queries(nc, pool, query_raw, "query")
+
+        n_banks = T // BANK
+        banks = [psum.tile([P, BANK], F32, name=f"bank{b}") for b in range(n_banks)]
+        for b in range(n_banks):
+            nc.tensor.matmul_mx(
+                out=banks[b][:],
+                lhsT=q2_codes[:].bitcast(FP8X4),
+                lhsT_scale=q2_scales[:],
+                rhs=tags[:, 2 * b * BANK : 2 * (b + 1) * BANK].bitcast(FP4X4),
+                rhs_scale=tags_plane[:, b * BANK : (b + 1) * BANK],
+                start=True,
+                stop=False,
+            )
+        scores = pool.tile([P, T], F32)
+        for b in range(n_banks):
+            h, c0 = divmod(b * BANK, T // 2)
+            nc.tensor.matmul_mx(
+                out=banks[b][:],
+                lhsT=q_codes[:].bitcast(FP8X4),
+                lhsT_scale=q_scales[:],
+                rhs=keys[h][:, c0 : c0 + BANK].bitcast(FP8X4),
+                rhs_scale=keys_plane[:, b * BANK : (b + 1) * BANK],
+                start=False,
+                stop=True,
+            )
+            cols = scores[:, b * BANK : (b + 1) * BANK]
+            if b % 2 == 0:
+                nc.scalar.activation(out=cols, in_=banks[b][:], func=ACT.Copy)
+            else:
+                nc.vector.tensor_copy(out=cols, in_=banks[b][:])
+
+        neg_lam = pool.tile([P, 1], F32)
+        nc.gpsimd.tensor_scalar(neg_lam[:], lam_col[:], -1.0, 0.0, ALU.mult, ALU.add)
+
+        list_cols = [slice(h * HALF // 16, (h + 1) * HALF // 16) for h in range(2)]
+        left = [pool.tile([P, HALF], F32, name=f"left{h}") for h in range(2)]
+        right = [pool.tile([P, HALF], F32, name=f"right{h}") for h in range(2)]
+        larger = [pool.tile([P, HALF], F32, name=f"larger{h}") for h in range(2)]
+        nc.vector.tensor_copy(left[0][:], scores[:].indirect(left_list[:, list_cols[0]]))
+        nc.scalar.activation(right[0][:], scores[:].indirect(right_list[:, list_cols[0]]), ACT.Copy)
+        nc.scalar.activation(left[1][:], scores[:].indirect(left_list[:, list_cols[1]]), ACT.Copy)
+        nc.scalar.activation(right[1][:], scores[:].indirect(right_list[:, list_cols[1]]), ACT.Copy)
+        for h in range(2):
+            nc.vector.tensor_tensor(larger[h][:], left[h][:], right[h][:], ALU.max)
+            nc.vector.tensor_copy(shadow[:].indirect(own_list[:, list_cols[h]]), larger[h][:])
+
+        diff = pool.tile([P, T], F32)
+        neg_top = pool.tile([P, 1], F32)
+        nc.vector.scalar_tensor_tensor(diff[:], shadow[:], neg_lam[:], scores[:], ALU.mult, ALU.add)
+        nc.vector.tensor_reduce(neg_top[:], diff[:], mybir.AxisListType.X, ALU.max, negate=True)
+
+        for h in range(2):
+            result = pool.tile([P, HALF], F32, name=f"result{h}")
+            nc.scalar.activation(
+                result[:], diff[:].indirect(out_list[:, list_cols[h]]), ACT.Exp, bias=neg_top[:]
+            )
+            nc.sync.dma_start(out=out[:, h * HALF : (h + 1) * HALF], in_=result[:])

@@ -16,14 +16,13 @@ ACT = mybir.ActivationFunctionType
 P = 128
 D, T, SLOTS, Q = 512, 1024, 512, 128
 PACK = 4
-BANK = 256
 HALF = SLOTS // 2
 FLOPS = 2 * 2 * D * Q * T
 
 
-def load_scale_rows(nc, plane, rows):
-    for quad in range(4):
-        nc.sync.dma_start(
+def load_scale_rows(queues, plane, rows):
+    for quad, queue in enumerate(queues):
+        queue.dma_start(
             out=plane[32 * quad : 32 * quad + 4, :].bitcast(I32),
             in_=rows[0, 4 * quad : 4 * quad + 4, :].bitcast(I32),
         )
@@ -61,7 +60,7 @@ def tile_attend_shadowed_parts_kernel(
         query_raw = pool.tile([P, PACK, Q], F32)
         query2_raw = pool.tile([P, PACK, Q], F32)
         tags = pool.tile([P, 2 * T], U8, align_bytes=64)
-        keys = [pool.tile([P, T // 2], U32, align_bytes=64, name=f"keys{h}") for h in range(2)]
+        keys = pool.tile([P, T], U32, align_bytes=64)
         keys_dram = keys_words[0].rearrange("p n t -> p (n t)").bitcast(I32)
         lists = [pool.tile([P, SLOTS // 16], U16, name=f"list{n}") for n in range(4)]
         own_list, left_list, right_list, out_list = lists
@@ -69,11 +68,10 @@ def tile_attend_shadowed_parts_kernel(
 
         nc.sync.dma_start(out=query2_raw[:], in_=query2.rearrange("(p t) c -> p t c", t=PACK))
         nc.sync.dma_start(out=tags[:].bitcast(I32), in_=tags_words[0].bitcast(I32))
-        load_scale_rows(nc, tags_plane, tags_scales)
+        load_scale_rows([nc.scalar, nc.sync, nc.scalar, nc.scalar], tags_plane, tags_scales)
         nc.sync.dma_start(out=query_raw[:], in_=query.rearrange("(p t) c -> p t c", t=PACK))
-        nc.sync.dma_start(out=keys[0][:].bitcast(I32), in_=keys_dram[:, : T // 2])
-        load_scale_rows(nc, keys_plane, keys_scales)
-        nc.sync.dma_start(out=keys[1][:].bitcast(I32), in_=keys_dram[:, T // 2 :])
+        nc.sync.dma_start(out=keys[:].bitcast(I32), in_=keys_dram)
+        load_scale_rows([nc.scalar] * 4, keys_plane, keys_scales)
         nc.sync.dma_start(left_list[:], offs2)
         nc.sync.dma_start(right_list[:], offs3)
         nc.sync.dma_start(own_list[:], offs)
@@ -83,35 +81,34 @@ def tile_attend_shadowed_parts_kernel(
         q2_codes, q2_scales = quantise_queries(nc, pool, query2_raw, "query2")
         q_codes, q_scales = quantise_queries(nc, pool, query_raw, "query")
 
-        n_banks = T // BANK
-        banks = [psum.tile([P, BANK], F32, name=f"bank{b}") for b in range(n_banks)]
-        for b in range(n_banks):
+        edges = [0, 256, 512, 768, 896, 1024]
+        spans = [slice(a, b) for a, b in zip(edges, edges[1:])]
+        banks = [psum.tile([P, s.stop - s.start], F32, name=f"bank{b}") for b, s in enumerate(spans)]
+        for bank, cols in zip(banks, spans):
             nc.tensor.matmul_mx(
-                out=banks[b][:],
+                out=bank[:],
                 lhsT=q2_codes[:].bitcast(FP8X4),
                 lhsT_scale=q2_scales[:],
-                rhs=tags[:, 2 * b * BANK : 2 * (b + 1) * BANK].bitcast(FP4X4),
-                rhs_scale=tags_plane[:, b * BANK : (b + 1) * BANK],
+                rhs=tags[:, 2 * cols.start : 2 * cols.stop].bitcast(FP4X4),
+                rhs_scale=tags_plane[:, cols],
                 start=True,
                 stop=False,
             )
         scores = pool.tile([P, T], F32)
-        for b in range(n_banks):
-            h, c0 = divmod(b * BANK, T // 2)
+        for b, (bank, cols) in enumerate(zip(banks, spans)):
             nc.tensor.matmul_mx(
-                out=banks[b][:],
+                out=bank[:],
                 lhsT=q_codes[:].bitcast(FP8X4),
                 lhsT_scale=q_scales[:],
-                rhs=keys[h][:, c0 : c0 + BANK].bitcast(FP8X4),
-                rhs_scale=keys_plane[:, b * BANK : (b + 1) * BANK],
+                rhs=keys[:, cols].bitcast(FP8X4),
+                rhs_scale=keys_plane[:, cols],
                 start=False,
                 stop=True,
             )
-            cols = scores[:, b * BANK : (b + 1) * BANK]
             if b % 2 == 0:
-                nc.scalar.activation(out=cols, in_=banks[b][:], func=ACT.Copy)
+                nc.scalar.activation(out=scores[:, cols], in_=bank[:], func=ACT.Copy)
             else:
-                nc.vector.tensor_copy(out=cols, in_=banks[b][:])
+                nc.vector.tensor_copy(out=scores[:, cols], in_=bank[:])
 
         neg_lam = pool.tile([P, 1], F32)
         nc.gpsimd.tensor_scalar(neg_lam[:], lam_col[:], -1.0, 0.0, ALU.mult, ALU.add)

@@ -16,30 +16,38 @@ ACT = mybir.ActivationFunctionType
 P = 128
 D, T, SLOTS, Q = 512, 1024, 512, 128
 PACK = 4
+QUADRANTS = 4
+PER_COLUMN = 16
 HALF = SLOTS // 2
+LEAD = HALF // 2
+BANK_EDGES = (0, 256, 512, 768, 896, 1024)
 FLOPS = 2 * 2 * D * Q * T
 
 
-def load_scale_rows(queues, plane, rows):
-    for quad, queue in enumerate(queues):
-        queue.dma_start(
-            out=plane[32 * quad : 32 * quad + 4, :].bitcast(I32),
-            in_=rows[0, 4 * quad : 4 * quad + 4, :].bitcast(I32),
+def entries(list_tile, start, stop):
+    return list_tile[:, start // PER_COLUMN : stop // PER_COLUMN]
+
+
+def load_scale_rows(nc, plane, rows):
+    for j in range(QUADRANTS):
+        nc.sync.dma_start(
+            out=plane[32 * j : 32 * j + 4, :].bitcast(I32),
+            in_=rows[0, 4 * j : 4 * j + 4, :].bitcast(I32),
         )
 
 
 def quantise_queries(nc, pool, raw, name):
     grouped = pool.tile([P, Q, PACK], BF16, align_bytes=64, name=name + "_bf16")
-    codes = pool.tile([P, Q], U32, align_bytes=64, name=name + "_codes")
-    scales = pool.tile([P, Q], U8, align_bytes=64, name=name + "_scales")
+    words = pool.tile([P, Q], U32, align_bytes=64, name=name + "_words")
+    plane = pool.tile([P, Q], U8, align_bytes=64, name=name + "_plane")
     nc.vector.tensor_copy(
-        out=grouped[:].rearrange("p (c i) t -> p c t i", i=4),
-        in_=raw[:].rearrange("p t (c i) -> p c t i", i=4),
+        out=grouped[:].rearrange("p (c i) r -> p c r i", i=4),
+        in_=raw[:].rearrange("p r (c i) -> p c r i", i=4),
     )
     nc.vector.quantize_mx(
-        out=codes[:].bitcast(FP8X4), scales=scales[:], in_=grouped[:].rearrange("p c t -> p (c t)")
+        out=words[:].bitcast(FP8X4), scales=plane[:], in_=grouped[:].rearrange("p c r -> p (c r)")
     )
-    return codes, scales
+    return words, plane
 
 
 def tile_attend_shadowed_parts_kernel(
@@ -52,43 +60,47 @@ def tile_attend_shadowed_parts_kernel(
 
         tags_plane = pool.tile([P, T], U8, align_bytes=64)
         keys_plane = pool.tile([P, T], U8, align_bytes=64)
-        shadow = pool.tile([P, T], F32)
+        placed = pool.tile([P, T], F32)
         nc.vector.memset(tags_plane[:].bitcast(I32), 0)
         nc.vector.memset(keys_plane[:].bitcast(I32), 0)
-        nc.vector.memset(shadow[:], 0.0)
+        nc.vector.memset(placed[:], 0.0)
 
         query_raw = pool.tile([P, PACK, Q], F32)
         query2_raw = pool.tile([P, PACK, Q], F32)
         tags = pool.tile([P, 2 * T], U8, align_bytes=64)
         keys = pool.tile([P, T], U32, align_bytes=64)
-        keys_dram = keys_words[0].rearrange("p n t -> p (n t)").bitcast(I32)
-        lists = [pool.tile([P, SLOTS // 16], U16, name=f"list{n}") for n in range(4)]
-        own_list, left_list, right_list, out_list = lists
+        own_list = pool.tile([P, SLOTS // PER_COLUMN], U16)
+        left_list = pool.tile([P, SLOTS // PER_COLUMN], U16)
+        right_list = pool.tile([P, SLOTS // PER_COLUMN], U16)
+        out_list = pool.tile([P, SLOTS // PER_COLUMN], U16)
         lam_col = pool.tile([P, 1], F32)
 
-        nc.sync.dma_start(out=query2_raw[:], in_=query2.rearrange("(p t) c -> p t c", t=PACK))
+        nc.sync.dma_start(out=query2_raw[:], in_=query2.rearrange("(p r) c -> p r c", r=PACK))
         nc.sync.dma_start(out=tags[:].bitcast(I32), in_=tags_words[0].bitcast(I32))
-        load_scale_rows([nc.scalar, nc.sync, nc.scalar, nc.scalar], tags_plane, tags_scales)
-        nc.sync.dma_start(out=query_raw[:], in_=query.rearrange("(p t) c -> p t c", t=PACK))
-        nc.sync.dma_start(out=keys[:].bitcast(I32), in_=keys_dram)
-        load_scale_rows([nc.scalar] * 4, keys_plane, keys_scales)
-        nc.sync.dma_start(left_list[:], offs2)
+        load_scale_rows(nc, tags_plane, tags_scales)
+        nc.sync.dma_start(out=query_raw[:], in_=query.rearrange("(p r) c -> p r c", r=PACK))
+        nc.sync.dma_start(
+            out=keys[:].bitcast(I32), in_=keys_words[0].rearrange("p n r -> p (n r)").bitcast(I32)
+        )
+        load_scale_rows(nc, keys_plane, keys_scales)
+        nc.sync.dma_start(out=lam_col[:], in_=lam)
         nc.sync.dma_start(right_list[:], offs3)
+        nc.sync.dma_start(left_list[:], offs2)
         nc.sync.dma_start(own_list[:], offs)
         nc.sync.dma_start(out_list[:], offs4)
-        nc.sync.dma_start(out=lam_col[:], in_=lam)
 
-        q2_codes, q2_scales = quantise_queries(nc, pool, query2_raw, "query2")
-        q_codes, q_scales = quantise_queries(nc, pool, query_raw, "query")
+        query2_words, query2_plane = quantise_queries(nc, pool, query2_raw, "query2")
+        query_words, query_plane = quantise_queries(nc, pool, query_raw, "query")
+        neg_lam = pool.tile([P, 1], F32)
+        nc.scalar.activation(neg_lam[:], lam_col[:], ACT.Copy, scale=-1.0)
 
-        edges = [0, 256, 512, 768, 896, 1024]
-        spans = [slice(a, b) for a, b in zip(edges, edges[1:])]
+        spans = [slice(lo, hi) for lo, hi in zip(BANK_EDGES, BANK_EDGES[1:])]
         banks = [psum.tile([P, s.stop - s.start], F32, name=f"bank{b}") for b, s in enumerate(spans)]
         for bank, cols in zip(banks, spans):
             nc.tensor.matmul_mx(
                 out=bank[:],
-                lhsT=q2_codes[:].bitcast(FP8X4),
-                lhsT_scale=q2_scales[:],
+                lhsT=query2_words[:].bitcast(FP8X4),
+                lhsT_scale=query2_plane[:],
                 rhs=tags[:, 2 * cols.start : 2 * cols.stop].bitcast(FP4X4),
                 rhs_scale=tags_plane[:, cols],
                 start=True,
@@ -98,8 +110,8 @@ def tile_attend_shadowed_parts_kernel(
         for b, (bank, cols) in enumerate(zip(banks, spans)):
             nc.tensor.matmul_mx(
                 out=bank[:],
-                lhsT=q_codes[:].bitcast(FP8X4),
-                lhsT_scale=q_scales[:],
+                lhsT=query_words[:].bitcast(FP8X4),
+                lhsT_scale=query_plane[:],
                 rhs=keys[:, cols].bitcast(FP8X4),
                 rhs_scale=keys_plane[:, cols],
                 start=False,
@@ -110,29 +122,29 @@ def tile_attend_shadowed_parts_kernel(
             else:
                 nc.vector.tensor_copy(out=scores[:, cols], in_=bank[:])
 
-        neg_lam = pool.tile([P, 1], F32)
-        nc.gpsimd.tensor_scalar(neg_lam[:], lam_col[:], -1.0, 0.0, ALU.mult, ALU.add)
-
-        list_cols = [slice(h * HALF // 16, (h + 1) * HALF // 16) for h in range(2)]
         left = [pool.tile([P, HALF], F32, name=f"left{h}") for h in range(2)]
         right = [pool.tile([P, HALF], F32, name=f"right{h}") for h in range(2)]
-        larger = [pool.tile([P, HALF], F32, name=f"larger{h}") for h in range(2)]
-        nc.vector.tensor_copy(left[0][:], scores[:].indirect(left_list[:, list_cols[0]]))
-        nc.scalar.activation(right[0][:], scores[:].indirect(right_list[:, list_cols[0]]), ACT.Copy)
-        nc.scalar.activation(left[1][:], scores[:].indirect(left_list[:, list_cols[1]]), ACT.Copy)
-        nc.scalar.activation(right[1][:], scores[:].indirect(right_list[:, list_cols[1]]), ACT.Copy)
-        for h in range(2):
-            nc.vector.tensor_tensor(larger[h][:], left[h][:], right[h][:], ALU.max)
-            nc.vector.tensor_copy(shadow[:].indirect(own_list[:, list_cols[h]]), larger[h][:])
+        nc.vector.tensor_copy(left[0][:], scores[:].indirect(entries(left_list, 0, HALF)))
+        nc.scalar.activation(right[0][:], scores[:].indirect(entries(right_list, 0, HALF)), ACT.Copy)
+        nc.scalar.activation(left[1][:], scores[:].indirect(entries(left_list, HALF, SLOTS)), ACT.Copy)
+        nc.scalar.activation(right[1][:], scores[:].indirect(entries(right_list, HALF, SLOTS)), ACT.Copy)
+
+        larger = pool.tile([P, SLOTS], F32)
+        nc.vector.tensor_tensor(larger[:, :LEAD], left[0][:, :LEAD], right[0][:, :LEAD], ALU.max)
+        nc.vector.tensor_tensor(larger[:, LEAD:HALF], left[0][:, LEAD:], right[0][:, LEAD:], ALU.max)
+        nc.vector.tensor_copy(placed[:].indirect(entries(own_list, 0, LEAD)), larger[:, :LEAD])
+        nc.vector.tensor_tensor(larger[:, HALF:], left[1][:], right[1][:], ALU.max)
+        nc.vector.tensor_copy(placed[:].indirect(entries(own_list, LEAD, SLOTS)), larger[:, LEAD:])
 
         diff = pool.tile([P, T], F32)
         neg_top = pool.tile([P, 1], F32)
-        nc.vector.scalar_tensor_tensor(diff[:], shadow[:], neg_lam[:], scores[:], ALU.mult, ALU.add)
+        nc.vector.scalar_tensor_tensor(diff[:], placed[:], neg_lam[:], scores[:], ALU.mult, ALU.add)
         nc.vector.tensor_reduce(neg_top[:], diff[:], mybir.AxisListType.X, ALU.max, negate=True)
 
         for h in range(2):
+            lo, hi = h * HALF, (h + 1) * HALF
             result = pool.tile([P, HALF], F32, name=f"result{h}")
             nc.scalar.activation(
-                result[:], diff[:].indirect(out_list[:, list_cols[h]]), ACT.Exp, bias=neg_top[:]
+                result[:], diff[:].indirect(entries(out_list, lo, hi)), ACT.Exp, bias=neg_top[:]
             )
-            nc.sync.dma_start(out=out[:, h * HALF : (h + 1) * HALF], in_=result[:])
+            nc.sync.dma_start(out=out[:, lo:hi], in_=result[:])

from contextlib import ExitStack

import concourse.mybir as mybir

F32 = mybir.dt.float32
BF16 = mybir.dt.bfloat16
I32 = mybir.dt.int32
U32 = mybir.dt.uint32
U16 = mybir.dt.uint16
U8 = mybir.dt.uint8
FP8X4 = mybir.dt.float8_e4m3fn_x4
FP4X4 = mybir.dt.float4_e2m1fn_x4
ALU = mybir.AluOpType
ACT = mybir.ActivationFunctionType

P = 128
D, T, SLOTS, Q = 512, 1024, 512, 128
PACK = 4
QUADRANTS = 4
PER_COLUMN = 16
HALF = SLOTS // 2
LEAD = HALF // 2
BANK_EDGES = (0, 256, 512, 768, 896, 1024)
FLOPS = 2 * 2 * D * Q * T


def entries(list_tile, start, stop):
    return list_tile[:, start // PER_COLUMN : stop // PER_COLUMN]


def load_scale_rows(nc, plane, rows):
    for j in range(QUADRANTS):
        nc.sync.dma_start(
            out=plane[32 * j : 32 * j + 4, :].bitcast(I32),
            in_=rows[0, 4 * j : 4 * j + 4, :].bitcast(I32),
        )


def quantise_queries(nc, pool, raw, name):
    grouped = pool.tile([P, Q, PACK], BF16, align_bytes=64, name=name + "_bf16")
    words = pool.tile([P, Q], U32, align_bytes=64, name=name + "_words")
    plane = pool.tile([P, Q], U8, align_bytes=64, name=name + "_plane")
    nc.vector.tensor_copy(
        out=grouped[:].rearrange("p (c i) r -> p c r i", i=4),
        in_=raw[:].rearrange("p r (c i) -> p c r i", i=4),
    )
    nc.vector.quantize_mx(
        out=words[:].bitcast(FP8X4), scales=plane[:], in_=grouped[:].rearrange("p c r -> p (c r)")
    )
    return words, plane


def tile_attend_shadowed_parts_kernel(
    tc, query, query2, keys_words, keys_scales, tags_words, tags_scales, lam, offs, offs2, offs3, offs4, out
):
    nc = tc.nc
    with ExitStack() as ctx:
        pool = ctx.enter_context(tc.tile_pool(name="sbuf", bufs=1))
        psum = ctx.enter_context(tc.psum_pool(name="psum", bufs=1))

        tags_plane = pool.tile([P, T], U8, align_bytes=64)
        keys_plane = pool.tile([P, T], U8, align_bytes=64)
        placed = pool.tile([P, T], F32)
        nc.vector.memset(tags_plane[:].bitcast(I32), 0)
        nc.vector.memset(keys_plane[:].bitcast(I32), 0)
        nc.vector.memset(placed[:], 0.0)

        query_raw = pool.tile([P, PACK, Q], F32)
        query2_raw = pool.tile([P, PACK, Q], F32)
        tags = pool.tile([P, 2 * T], U8, align_bytes=64)
        keys = pool.tile([P, T], U32, align_bytes=64)
        own_list = pool.tile([P, SLOTS // PER_COLUMN], U16)
        left_list = pool.tile([P, SLOTS // PER_COLUMN], U16)
        right_list = pool.tile([P, SLOTS // PER_COLUMN], U16)
        out_list = pool.tile([P, SLOTS // PER_COLUMN], U16)
        lam_col = pool.tile([P, 1], F32)

        nc.sync.dma_start(out=query2_raw[:], in_=query2.rearrange("(p r) c -> p r c", r=PACK))
        nc.sync.dma_start(out=tags[:].bitcast(I32), in_=tags_words[0].bitcast(I32))
        load_scale_rows(nc, tags_plane, tags_scales)
        nc.sync.dma_start(out=query_raw[:], in_=query.rearrange("(p r) c -> p r c", r=PACK))
        nc.sync.dma_start(
            out=keys[:].bitcast(I32), in_=keys_words[0].rearrange("p n r -> p (n r)").bitcast(I32)
        )
        load_scale_rows(nc, keys_plane, keys_scales)
        nc.sync.dma_start(out=lam_col[:], in_=lam)
        nc.sync.dma_start(right_list[:], offs3)
        nc.sync.dma_start(left_list[:], offs2)
        nc.sync.dma_start(own_list[:], offs)
        nc.sync.dma_start(out_list[:], offs4)

        query2_words, query2_plane = quantise_queries(nc, pool, query2_raw, "query2")
        query_words, query_plane = quantise_queries(nc, pool, query_raw, "query")
        neg_lam = pool.tile([P, 1], F32)
        nc.scalar.activation(neg_lam[:], lam_col[:], ACT.Copy, scale=-1.0)

        spans = [slice(lo, hi) for lo, hi in zip(BANK_EDGES, BANK_EDGES[1:])]
        banks = [psum.tile([P, s.stop - s.start], F32, name=f"bank{b}") for b, s in enumerate(spans)]
        for bank, cols in zip(banks, spans):
            nc.tensor.matmul_mx(
                out=bank[:],
                lhsT=query2_words[:].bitcast(FP8X4),
                lhsT_scale=query2_plane[:],
                rhs=tags[:, 2 * cols.start : 2 * cols.stop].bitcast(FP4X4),
                rhs_scale=tags_plane[:, cols],
                start=True,
                stop=False,
            )
        scores = pool.tile([P, T], F32)
        for b, (bank, cols) in enumerate(zip(banks, spans)):
            nc.tensor.matmul_mx(
                out=bank[:],
                lhsT=query_words[:].bitcast(FP8X4),
                lhsT_scale=query_plane[:],
                rhs=keys[:, cols].bitcast(FP8X4),
                rhs_scale=keys_plane[:, cols],
                start=False,
                stop=True,
            )
            if b % 2 == 0:
                nc.scalar.activation(out=scores[:, cols], in_=bank[:], func=ACT.Copy)
            else:
                nc.vector.tensor_copy(out=scores[:, cols], in_=bank[:])

        left = [pool.tile([P, HALF], F32, name=f"left{h}") for h in range(2)]
        right = [pool.tile([P, HALF], F32, name=f"right{h}") for h in range(2)]
        nc.vector.tensor_copy(left[0][:], scores[:].indirect(entries(left_list, 0, HALF)))
        nc.scalar.activation(right[0][:], scores[:].indirect(entries(right_list, 0, HALF)), ACT.Copy)
        nc.scalar.activation(left[1][:], scores[:].indirect(entries(left_list, HALF, SLOTS)), ACT.Copy)
        nc.scalar.activation(right[1][:], scores[:].indirect(entries(right_list, HALF, SLOTS)), ACT.Copy)

        larger = pool.tile([P, SLOTS], F32)
        nc.vector.tensor_tensor(larger[:, :LEAD], left[0][:, :LEAD], right[0][:, :LEAD], ALU.max)
        nc.vector.tensor_tensor(larger[:, LEAD:HALF], left[0][:, LEAD:], right[0][:, LEAD:], ALU.max)
        nc.vector.tensor_copy(placed[:].indirect(entries(own_list, 0, LEAD)), larger[:, :LEAD])
        nc.vector.tensor_tensor(larger[:, HALF:], left[1][:], right[1][:], ALU.max)
        nc.vector.tensor_copy(placed[:].indirect(entries(own_list, LEAD, SLOTS)), larger[:, LEAD:])

        diff = pool.tile([P, T], F32)
        neg_top = pool.tile([P, 1], F32)
        nc.vector.scalar_tensor_tensor(diff[:], placed[:], neg_lam[:], scores[:], ALU.mult, ALU.add)
        nc.vector.tensor_reduce(neg_top[:], diff[:], mybir.AxisListType.X, ALU.max, negate=True)

        for h in range(2):
            lo, hi = h * HALF, (h + 1) * HALF
            result = pool.tile([P, HALF], F32, name=f"result{h}")
            nc.scalar.activation(
                result[:], diff[:].indirect(entries(out_list, lo, hi)), ACT.Exp, bias=neg_top[:]
            )
            nc.sync.dma_start(out=out[:, lo:hi], in_=result[:])
